import numpy as np
import ml_dtypes


def mxq(x, axis, fmt="e4m3"):
    dtype, down = {"e4m3": (ml_dtypes.float8_e4m3fn, 7), "e5m2": (ml_dtypes.float8_e5m2, 14)}[fmt]
    v = np.moveaxis(np.asarray(x, np.float32).astype(ml_dtypes.bfloat16).astype(np.float64), axis, -1)
    blocks = v.reshape(v.shape[:-1] + (-1, 32))
    amax = np.abs(blocks).max(-1, keepdims=True)
    byte = np.maximum(np.where(amax > 0, np.frexp(amax)[1] - 1 + 127, 0) - down, 1)
    scale = np.exp2(byte - 127.0)
    codes = (blocks / scale).astype(np.float32).astype(dtype).astype(np.float64)
    return np.moveaxis((codes * scale).reshape(v.shape), -1, axis)


WIDE = False


def mx_kscale(k):
    if not WIDE:
        return np.ones(k)
    levels = np.array([10, -10, 5, -5, 0])
    if k % 512:
        return np.exp2(np.random.permutation(np.resize(levels, k // 32))).repeat(32)
    a = np.empty((k // 512, 16))
    for p in range(k // 512):
        a[p, :8] = np.random.permutation(np.resize(levels, 8))
        for g in range(8):
            far = levels[np.abs(levels - a[p, g]) >= 10]
            a[p, g + 8] = far[np.random.randint(len(far))]
    return np.exp2(a.ravel()).repeat(32)


def f64(x):
    return np.asarray(x).astype(np.float64)


def striped(idx):
    return np.tile(idx.reshape(-1, 16).T, (8, 1)).astype(np.uint16)


def unstriped(offs):
    return offs[:16].T.reshape(-1).astype(np.int64)


def striped8(idx):
    return np.concatenate([x.reshape(-1, 16).T for x in idx]).astype(np.uint16)


def runs(offs, k):
    lists = np.stack([offs[16 * r : 16 * r + 16].T.reshape(-1) for r in range(8)]).astype(np.int64)
    return lists[np.arange(k) % 512 // 64]


def pack_weight(w):
    k, n = w.shape
    w = f64(np.asarray(w, np.float32).astype(ml_dtypes.bfloat16)).reshape(k // 32, 32, n)
    amax = np.abs(w).max(1)
    byte = np.clip(np.where(amax > 0, np.frexp(amax)[1] - 1 + 127 - 7, 1), 1, 254)
    scaled = (w * np.exp2(127.0 - byte)[:, None, :]).reshape(k, n).astype(np.float32)
    words = np.ascontiguousarray(scaled.reshape(k // 512, 128, 4, n).transpose(0, 1, 3, 2)).astype(ml_dtypes.float8_e4m3fn).view(np.uint8)
    return words, np.ascontiguousarray(byte.astype(np.uint8).reshape(k // 512, 16, n))


def unpack_weight(words, scales):
    g, p, n, _ = words.shape
    vals = np.ascontiguousarray(words).view(ml_dtypes.float8_e4m3fn).astype(np.float64) * np.repeat(np.exp2(scales.astype(np.float64) - 127.0), 8, axis=1)[..., None]
    return vals.transpose(0, 1, 3, 2).reshape(g * 512, n)

def planes(y):
    n, m = y.shape
    v = y.astype(np.float32).astype(ml_dtypes.bfloat16).astype(np.float64).reshape(n // 32, 32, m)
    top = np.abs(v).max(1)
    byte = np.clip(np.where(top > 0, np.frexp(top)[1] - 1 + 127 - 7, 1), 1, 254)
    codes = (v * np.exp2(127.0 - byte)[:, None, :]).reshape(n, m).astype(np.float32).astype(ml_dtypes.float8_e4m3fn).view(np.uint8)
    words = codes.reshape(n // 512, 128, 4, m).transpose(0, 1, 3, 2)
    return np.ascontiguousarray(words), np.ascontiguousarray(byte.astype(np.uint8).reshape(n // 512, 16, m))


K, T, S, G, H, C = 512, 1024, 256, 2048, 512, 512


def setup_inputs():
    n = np.random.standard_normal
    s = mx_kscale(K)[:, None]
    packed_xT = pack_weight(n((K, T)) * s)
    packed_dT = pack_weight(n((K, G)) / s)
    return {
        "x_words": packed_xT[0],
        "x_scales": packed_xT[1],
        "d_words": packed_dT[0],
        "d_scales": packed_dT[1],
        "gs": (np.random.uniform(0.5, 1.5, (K, 1)) / s).astype(np.float32),
        "offs": striped(np.random.permutation(T)[:S]),
        "ka": striped8(np.random.randint(0, G, (8, H))),
        "kb": striped8(np.random.randint(0, G, (8, H))),
        "cand": striped(np.random.permutation(T)[:C]),
        "n1": striped(np.random.permutation(S)),
        "n2": striped(np.random.permutation(S)),
    }


def reference(x_words, x_scales, d_words, d_scales, gs, offs, ka, kb, cand, n1, n2):
    x_cand = unpack_weight(x_words, x_scales)[:, unstriped(cand)]
    d_ka = unpack_weight(d_words, d_scales)[np.arange(K)[:, None], runs(ka, K)]
    xq = unpack_weight(x_words, x_scales)[:, unstriped(offs)]
    d_kb = unpack_weight(d_words, d_scales)[np.arange(K)[:, None], runs(kb, K)]
    h = 0.0625 * (d_ka.T @ xq + d_kb.T @ xq)
    z = f64(gs) * h
    s = 0.0625 * ((x_cand.T @ mxq(z, 0, "e4m3")))
    ds = np.zeros((C, S))
    ds[:, unstriped(n1)] = s
    ds2 = np.zeros((C, S))
    ds2[:, unstriped(n2)] = s
    out_0 = np.maximum(ds, ds2)
    return (out_0,) + planes(out_0)

@@ -1,0 +1,202 @@
+from contextlib import ExitStack
+
+import concourse.mybir as mybir
+from concourse.masks import make_identity
+
+K, T, S, G, H, C = 512, 1024, 256, 2048, 512, 512
+FLOPS = 2 * (2 * K * H * S) + 2 * H * C * S
+
+F32 = mybir.dt.float32
+BF16 = mybir.dt.bfloat16
+I32 = mybir.dt.int32
+U32 = mybir.dt.uint32
+U16 = mybir.dt.uint16
+U8 = mybir.dt.uint8
+FP8X4 = mybir.dt.float8_e4m3fn_x4
+MULT = mybir.AluOpType.mult
+MAX = mybir.AluOpType.max
+COPY = mybir.ActivationFunctionType.Copy
+
+P = 128
+PACK = 4
+HALF = S // 2
+SIXTEENTH = 0.0625
+
+
+def tile_picked_aqcisendtwo_none_po_kernel(
+    tc, x_words, x_scales, d_words, d_scales, gs, offs, ka, kb, cand, n1, n2, out_0, out_1, out_2
+):
+    nc = tc.nc
+    with ExitStack() as ctx:
+        lists = ctx.enter_context(tc.tile_pool(name="lists", bufs=1))
+        keep = ctx.enter_context(tc.tile_pool(name="keep", bufs=1))
+        reuse = ctx.enter_context(tc.tile_pool(name="reuse", bufs=1))
+        psum = ctx.enter_context(tc.psum_pool(name="psum", bufs=1))
+
+        def load_list(src, name):
+            tile = lists.tile([P, src.shape[1]], U16, name=name)
+            nc.sync.dma_start(tile[:], src)
+            return tile
+
+        def entries(tile, start, count):
+            return tile[:, start // 16 : (start + count) // 16]
+
+        d_byte_table = reuse.tile([P, G], U8, align_bytes=64, offset=10240)
+        x_block_table = keep.tile([P, T], U8, align_bytes=64)
+        d_plane = keep.tile([P, 2 * H + HALF], U8, align_bytes=64)
+        nc.vector.memset(d_plane[:].bitcast(I32), 0)
+
+        ka_list = load_list(ka, "ka_list")
+        nc.sync.dma_start(d_byte_table[:].bitcast(I32), d_scales[0].bitcast(I32).unsqueeze(1).to_broadcast([16, 8, G // 4]))
+        kb_list = load_list(kb, "kb_list")
+        nc.sync.dma_start(x_block_table[:].bitcast(I32), x_scales[0].bitcast(I32).unsqueeze(1).to_broadcast([16, 8, T // 4]))
+        offs_list = load_list(offs, "offs_list")
+        x_word_table = keep.tile([P, T], U32, align_bytes=64)
+        d_word_table = reuse.tile([P, G], U32, align_bytes=64, offset=0)
+        nc.sync.dma_start(x_word_table[:].bitcast(I32), x_words[0].rearrange("p n t -> p (n t)").bitcast(I32))
+        nc.sync.dma_start(d_word_table[:].bitcast(I32), d_words[0].rearrange("p n t -> p (n t)").bitcast(I32))
+        cand_list = load_list(cand, "cand_list")
+        n_lists = [load_list(n1, "n1_list"), load_list(n2, "n2_list")]
+        gs4 = keep.tile([P, PACK], F32)
+        nc.gpsimd.dma_start(gs4[:], gs.rearrange("(p t) o -> p (t o)", t=PACK))
+        ident = keep.tile([P, P], F32)
+        make_identity(nc, ident[:])
+
+        d_bytes = keep.tile([P, 2 * H + HALF], U8, align_bytes=64)
+        nc.vector.tensor_copy(d_bytes[:, 0:H], d_byte_table[:].indirect(ka_list[:]))
+        nc.vector.tensor_copy(d_bytes[:, H : 2 * H], d_byte_table[:].indirect(kb_list[:]))
+        nc.vector.tensor_copy(d_bytes[:, 2 * H : 2 * H + HALF], x_block_table[:].indirect(entries(offs_list, 0, HALF)))
+        for q in range(4):
+            queue = nc.scalar if q % 2 else nc.sync
+            queue.dma_start(
+                d_plane[32 * q : 32 * q + 4, :].bitcast(I32), d_bytes[32 * q : 32 * q + 32 : 8, :].bitcast(I32)
+            )
+
+        x_byte_table = reuse.tile([P, T], U8, align_bytes=64, offset=10240)
+        for q in range(4):
+            nc.sync.dma_start(
+                x_byte_table[32 * q : 32 * q + 32, :].bitcast(I32),
+                x_scales[0, 4 * q : 4 * q + 4, :].bitcast(I32).unsqueeze(0).to_broadcast([8, 4, T // 4]),
+            )
+
+        def gather_token_bytes(half, tile):
+            nc.vector.tensor_copy(tile[:], x_byte_table[:].indirect(entries(offs_list, half * HALF, HALF)))
+
+        def gather_token_words(half, tile):
+            nc.vector.tensor_copy(tile[:], x_word_table[:].indirect(entries(offs_list, half * HALF, HALF)))
+
+        xq_words0 = keep.tile([P, HALF], U32, align_bytes=64)
+        gather_token_words(0, xq_words0)
+        xq_words1 = keep.tile([P, HALF], U32, align_bytes=64)
+        gather_token_words(1, xq_words1)
+
+        da_words = keep.tile([P, H], U32, align_bytes=64)
+        db_words = keep.tile([P, H], U32, align_bytes=64)
+        nc.vector.tensor_copy(da_words[:], d_word_table[:].indirect(ka_list[:]))
+        for part in range(2):
+            nc.vector.tensor_copy(
+                db_words[:, part * 256 : (part + 1) * 256], d_word_table[:].indirect(entries(kb_list, part * 256, 256))
+            )
+
+        def first_product(bank, words, scale_bytes, lo, n):
+            nc.tensor.matmul_mx(
+                bank[:, 0:n], lhsT=words[:].bitcast(FP8X4), lhsT_scale=scale_bytes,
+                rhs=da_words[:, lo : lo + n].bitcast(FP8X4), rhs_scale=d_plane[:, lo : lo + n], start=True, stop=False,
+            )
+            nc.tensor.matmul_mx(
+                bank[:, 0:n], lhsT=words[:].bitcast(FP8X4), lhsT_scale=scale_bytes,
+                rhs=db_words[:, lo : lo + n].bitcast(FP8X4), rhs_scale=d_plane[:, H + lo : H + lo + n],
+                start=False, stop=True,
+            )
+
+        h_sorted0 = keep.tile([P, PACK, P], F32)
+        for part in range(2):
+            bank = psum.tile([P, 256], F32, name="h_bank%d" % part)
+            first_product(bank, xq_words0, d_plane[:, 2 * H : 2 * H + HALF], part * 256, 256)
+            nc.scalar.activation(
+                h_sorted0[:, :, part * 64 : (part + 1) * 64], bank[:].rearrange("j (p t) -> j t p", t=PACK),
+                COPY, scale=SIXTEENTH,
+            )
+
+        c_bytes = reuse.tile([P, C], U8, align_bytes=64, offset=2048)
+        c_words = reuse.tile([P, C], U32, align_bytes=64, offset=0)
+        nc.vector.tensor_copy(c_words[:].rearrange("p (t m) -> p m t", t=PACK), x_word_table[:].indirect(cand_list[:]))
+        nc.vector.tensor_copy(c_bytes[:].rearrange("p (t m) -> p m t", t=PACK), x_byte_table[:].indirect(cand_list[:]))
+
+        gs_spread = gs4[:].unsqueeze(1).to_broadcast([P, HALF, PACK])
+
+        def turn_and_quantise(half, h_sorted, z_bf, z_words, z_bytes):
+            turned = psum.tile([P, PACK, HALF], F32, name="turned%d" % half)
+            for t in range(PACK):
+                nc.tensor.transpose(turned[:, t, :], h_sorted[:, t, :], ident[:])
+            nc.vector.tensor_tensor(
+                z_bf[:].rearrange("p (j t) -> p j t", t=PACK), turned[:].rearrange("p t j -> p j t"), gs_spread, MULT
+            )
+            nc.vector.quantize_mx(z_words[:].bitcast(FP8X4), z_bytes[:], z_bf[:])
+
+        def second_product(out, t, z_words, z_bytes):
+            nc.tensor.matmul_mx(
+                out, lhsT=c_words[:, t * P : (t + 1) * P].bitcast(FP8X4), lhsT_scale=c_bytes[:, t * P : (t + 1) * P],
+                rhs=z_words[:].bitcast(FP8X4), rhs_scale=z_bytes[:], start=True, stop=True,
+            )
+
+        ds = [[keep.tile([P, S], F32, name="ds%d_%d" % (t, w)) for w in range(2)] for t in range(PACK)]
+
+        def scatter(half, t, values):
+            for w in range(2):
+                nc.scalar.activation(ds[t][w][:].indirect(entries(n_lists[w], half * HALF, HALF)), values, COPY)
+
+        z_bf0 = reuse.tile([P, PACK * HALF], BF16, align_bytes=64, offset=8192)
+        z_words0 = keep.tile([P, HALF], U32, align_bytes=64)
+        z_bytes0 = keep.tile([P, HALF], U8, align_bytes=64)
+        turn_and_quantise(0, h_sorted0, z_bf0, z_words0, z_bytes0)
+        s_first = psum.tile([P, HALF], F32, tag="shared_bank")
+        s_rest = psum.tile([P, PACK - 1, HALF], F32)
+        second_product(s_first[:], 0, z_words0, z_bytes0)
+        for t in range(1, PACK):
+            second_product(s_rest[:, t - 1, :], t, z_words0, z_bytes0)
+        s0 = keep.tile([P, PACK, HALF], F32)
+        nc.vector.tensor_scalar_mul(s0[:, 0, :], s_first[:], SIXTEENTH)
+        nc.vector.tensor_scalar_mul(s0[:, 1:PACK, :], s_rest[:], SIXTEENTH)
+        for t in range(PACK):
+            scatter(0, t, s0[:, t, :])
+
+        xq_bytes1 = reuse.tile([P, HALF], U8, align_bytes=64, offset=8192)
+        gather_token_bytes(1, xq_bytes1)
+        h_bank2 = psum.tile([P, H], F32, tag="shared_bank")
+        first_product(h_bank2, xq_words1, xq_bytes1[:], 0, H)
+        h_sorted1 = keep.tile([P, PACK, P], F32)
+        nc.vector.tensor_scalar_mul(h_sorted1[:], h_bank2[:].rearrange("j (p t) -> j t p", t=PACK), SIXTEENTH)
+        z_bf1 = keep.tile([P, PACK * HALF], BF16, align_bytes=64)
+        z_words1 = keep.tile([P, HALF], U32, align_bytes=64)
+        z_bytes1 = keep.tile([P, HALF], U8, align_bytes=64)
+        turn_and_quantise(1, h_sorted1, z_bf1, z_words1, z_bytes1)
+        s_second = psum.tile([P, PACK, HALF], F32)
+        for t in range(PACK):
+            second_product(s_second[:, t, :], t, z_words1, z_bytes1)
+        s1 = keep.tile([P, PACK, HALF], F32)
+        nc.vector.tensor_scalar_mul(s1[:], s_second[:], SIXTEENTH)
+
+        y_bf = keep.tile([P, S * PACK], BF16, align_bytes=64)
+        y_dealt = y_bf[:].rearrange("p (c t) -> p c t", t=PACK)
+        out_rows = out_0.rearrange("(p t) c -> p t c", t=PACK)
+        halves = [slice(0, HALF), slice(HALF, S)]
+        for t in range(PACK):
+            scatter(1, t, s1[:, t, :])
+            y = keep.tile([P, S], F32, name="y%d" % t)
+            for cols in halves:
+                nc.vector.tensor_tensor(y[:, cols], ds[t][0][:, cols], ds[t][1][:, cols], MAX)
+            nc.sync.dma_start(out_rows[:, t, :], y[:])
+            for cols in halves:
+                nc.vector.tensor_copy(y_dealt[:, cols, t], y[:, cols])
+
+        y_words = keep.tile([P, S], U32, align_bytes=64)
+        y_bytes = keep.tile([P, S], U8, align_bytes=64)
+        for cols in halves:
+            nc.vector.quantize_mx(
+                y_words[:, cols].bitcast(FP8X4), y_bytes[:, cols], y_bf[:, PACK * cols.start : PACK * cols.stop]
+            )
+        nc.sync.dma_start(out_1[0].rearrange("p n t -> p (n t)").bitcast(I32), y_words[:].bitcast(I32))
+        for q in range(4):
+            queue = nc.scalar if q < 2 else nc.sync
+            queue.dma_start(out_2[0, 4 * q : 4 * q + 4, :].bitcast(I32), y_bytes[32 * q : 32 * q + 4, :].bitcast(I32))

@@ -20,6 +20,7 @@ COPY = mybir.ActivationFunctionType.Copy
 P = 128
 PACK = 4
 HALF = S // 2
+QUARTER = S // 4
 SIXTEENTH = 0.0625
 
 
@@ -41,8 +42,8 @@ def tile_picked_aqcisendtwo_none_po_kernel(
         def entries(tile, start, count):
             return tile[:, start // 16 : (start + count) // 16]
 
-        d_byte_table = reuse.tile([P, G], U8, align_bytes=64, offset=10240)
-        x_block_table = keep.tile([P, T], U8, align_bytes=64)
+        d_byte_table = keep.tile([P, G], U8, align_bytes=64)
+        x_block_table = reuse.tile([P, T], U8, align_bytes=64, offset=10240)
         d_plane = keep.tile([P, 2 * H + HALF], U8, align_bytes=64)
         nc.vector.memset(d_plane[:].bitcast(I32), 0)
 
@@ -123,43 +124,52 @@ def tile_picked_aqcisendtwo_none_po_kernel(
         nc.vector.tensor_copy(c_words[:].rearrange("p (t m) -> p m t", t=PACK), x_word_table[:].indirect(cand_list[:]))
         nc.vector.tensor_copy(c_bytes[:].rearrange("p (t m) -> p m t", t=PACK), x_byte_table[:].indirect(cand_list[:]))
 
-        gs_spread = gs4[:].unsqueeze(1).to_broadcast([P, HALF, PACK])
-
-        def turn_and_quantise(half, h_sorted, z_bf, z_words, z_bytes):
+        def turn_and_quantise(half, h_sorted, z_bf, z_words, z_bytes, width):
             turned = psum.tile([P, PACK, HALF], F32, name="turned%d" % half)
             for t in range(PACK):
                 nc.tensor.transpose(turned[:, t, :], h_sorted[:, t, :], ident[:])
-            nc.vector.tensor_tensor(
-                z_bf[:].rearrange("p (j t) -> p j t", t=PACK), turned[:].rearrange("p t j -> p j t"), gs_spread, MULT
-            )
-            nc.vector.quantize_mx(z_words[:].bitcast(FP8X4), z_bytes[:], z_bf[:])
+            gs_spread = gs4[:].unsqueeze(1).to_broadcast([P, width, PACK])
+            for lo in range(0, HALF, width):
+                nc.vector.tensor_tensor(
+                    z_bf[:, PACK * lo : PACK * (lo + width)].rearrange("p (j t) -> p j t", t=PACK),
+                    turned[:, :, lo : lo + width].rearrange("p t j -> p j t"), gs_spread, MULT,
+                )
+            for lo in range(0, HALF, width):
+                nc.vector.quantize_mx(
+                    z_words[:, lo : lo + width].bitcast(FP8X4), z_bytes[:, lo : lo + width],
+                    z_bf[:, PACK * lo : PACK * (lo + width)],
+                )
 
-        def second_product(out, t, z_words, z_bytes):
+        def second_product(out, t, z_words, z_bytes, cols):
             nc.tensor.matmul_mx(
                 out, lhsT=c_words[:, t * P : (t + 1) * P].bitcast(FP8X4), lhsT_scale=c_bytes[:, t * P : (t + 1) * P],
-                rhs=z_words[:].bitcast(FP8X4), rhs_scale=z_bytes[:], start=True, stop=True,
+                rhs=z_words[:, cols].bitcast(FP8X4), rhs_scale=z_bytes[:, cols], start=True, stop=True,
             )
 
         ds = [[keep.tile([P, S], F32, name="ds%d_%d" % (t, w)) for w in range(2)] for t in range(PACK)]
 
-        def scatter(half, t, values):
+        def scatter(t, values, start, count):
             for w in range(2):
-                nc.scalar.activation(ds[t][w][:].indirect(entries(n_lists[w], half * HALF, HALF)), values, COPY)
+                nc.scalar.activation(ds[t][w][:].indirect(entries(n_lists[w], start, count)), values, COPY)
 
         z_bf0 = reuse.tile([P, PACK * HALF], BF16, align_bytes=64, offset=8192)
         z_words0 = keep.tile([P, HALF], U32, align_bytes=64)
         z_bytes0 = keep.tile([P, HALF], U8, align_bytes=64)
-        turn_and_quantise(0, h_sorted0, z_bf0, z_words0, z_bytes0)
-        s_first = psum.tile([P, HALF], F32, tag="shared_bank")
-        s_rest = psum.tile([P, PACK - 1, HALF], F32)
-        second_product(s_first[:], 0, z_words0, z_bytes0)
-        for t in range(1, PACK):
-            second_product(s_rest[:, t - 1, :], t, z_words0, z_bytes0)
+        turn_and_quantise(0, h_sorted0, z_bf0, z_words0, z_bytes0, QUARTER)
         s0 = keep.tile([P, PACK, HALF], F32)
-        nc.vector.tensor_scalar_mul(s0[:, 0, :], s_first[:], SIXTEENTH)
+        s_lead = [psum.tile([P, QUARTER], F32, name="s_lead0", tag="shared_bank"), psum.tile([P, QUARTER], F32, name="s_lead1")]
+        s_rest = psum.tile([P, PACK - 1, HALF], F32)
+        for u in range(2):
+            second_product(s_lead[u][:], 0, z_words0, z_bytes0, slice(u * QUARTER, (u + 1) * QUARTER))
+        for t in range(1, PACK):
+            second_product(s_rest[:, t - 1, :], t, z_words0, z_bytes0, slice(0, HALF))
+        for u in range(2):
+            nc.vector.tensor_scalar_mul(s0[:, 0, u * QUARTER : (u + 1) * QUARTER], s_lead[u][:], SIXTEENTH)
         nc.vector.tensor_scalar_mul(s0[:, 1:PACK, :], s_rest[:], SIXTEENTH)
-        for t in range(PACK):
-            scatter(0, t, s0[:, t, :])
+        for u in range(2):
+            scatter(0, s0[:, 0, u * QUARTER : (u + 1) * QUARTER], u * QUARTER, QUARTER)
+        for t in range(1, PACK):
+            scatter(t, s0[:, t, :], 0, HALF)
 
         xq_bytes1 = reuse.tile([P, HALF], U8, align_bytes=64, offset=8192)
         gather_token_bytes(1, xq_bytes1)
@@ -170,19 +180,20 @@ def tile_picked_aqcisendtwo_none_po_kernel(
         z_bf1 = keep.tile([P, PACK * HALF], BF16, align_bytes=64)
         z_words1 = keep.tile([P, HALF], U32, align_bytes=64)
         z_bytes1 = keep.tile([P, HALF], U8, align_bytes=64)
-        turn_and_quantise(1, h_sorted1, z_bf1, z_words1, z_bytes1)
+        turn_and_quantise(1, h_sorted1, z_bf1, z_words1, z_bytes1, HALF)
         s_second = psum.tile([P, PACK, HALF], F32)
         for t in range(PACK):
-            second_product(s_second[:, t, :], t, z_words1, z_bytes1)
+            second_product(s_second[:, t, :], t, z_words1, z_bytes1, slice(0, HALF))
         s1 = keep.tile([P, PACK, HALF], F32)
-        nc.vector.tensor_scalar_mul(s1[:], s_second[:], SIXTEENTH)
+        nc.vector.tensor_scalar_mul(s1[:, 0, :], s_second[:, 0, :], SIXTEENTH)
+        nc.vector.tensor_scalar_mul(s1[:, 1:PACK, :], s_second[:, 1:PACK, :], SIXTEENTH)
 
         y_bf = keep.tile([P, S * PACK], BF16, align_bytes=64)
         y_dealt = y_bf[:].rearrange("p (c t) -> p c t", t=PACK)
         out_rows = out_0.rearrange("(p t) c -> p t c", t=PACK)
         halves = [slice(0, HALF), slice(HALF, S)]
         for t in range(PACK):
-            scatter(1, t, s1[:, t, :])
+            scatter(t, s1[:, t, :], HALF, HALF)
             y = keep.tile([P, S], F32, name="y%d" % t)
             for cols in halves:
                 nc.vector.tensor_tensor(y[:, cols], ds[t][0][:, cols], ds[t][1][:, cols], MAX)
@@ -196,7 +207,9 @@ def tile_picked_aqcisendtwo_none_po_kernel(
             nc.vector.quantize_mx(
                 y_words[:, cols].bitcast(FP8X4), y_bytes[:, cols], y_bf[:, PACK * cols.start : PACK * cols.stop]
             )
-        nc.sync.dma_start(out_1[0].rearrange("p n t -> p (n t)").bitcast(I32), y_words[:].bitcast(I32))
+            nc.sync.dma_start(
+                out_1[0].rearrange("p n t -> p (n t)").bitcast(I32)[:, cols], y_words[:, cols].bitcast(I32)
+            )
         for q in range(4):
             queue = nc.scalar if q < 2 else nc.sync
             queue.dma_start(out_2[0, 4 * q : 4 * q + 4, :].bitcast(I32), y_bytes[32 * q : 32 * q + 4, :].bitcast(I32))

@@ -47,8 +47,8 @@ def tile_picked_aqcisendtwo_none_po_kernel(
         d_plane = keep.tile([P, 2 * H + HALF], U8, align_bytes=64)
         nc.vector.memset(d_plane[:].bitcast(I32), 0)
 
-        ka_list = load_list(ka, "ka_list")
         nc.sync.dma_start(d_byte_table[:].bitcast(I32), d_scales[0].bitcast(I32).unsqueeze(1).to_broadcast([16, 8, G // 4]))
+        ka_list = load_list(ka, "ka_list")
         kb_list = load_list(kb, "kb_list")
         nc.sync.dma_start(x_block_table[:].bitcast(I32), x_scales[0].bitcast(I32).unsqueeze(1).to_broadcast([16, 8, T // 4]))
         offs_list = load_list(offs, "offs_list")
@@ -112,7 +112,7 @@ def tile_picked_aqcisendtwo_none_po_kernel(
 
         h_sorted0 = keep.tile([P, PACK, P], F32)
         for part in range(2):
-            bank = psum.tile([P, 256], F32, name="h_bank%d" % part)
+            bank = psum.tile([P, 256], F32, name="h_bank%d" % part, tag="h_part%d" % part)
             first_product(bank, xq_words0, d_plane[:, 2 * H : 2 * H + HALF], part * 256, 256)
             nc.scalar.activation(
                 h_sorted0[:, :, part * 64 : (part + 1) * 64], bank[:].rearrange("j (p t) -> j t p", t=PACK),
@@ -176,17 +176,22 @@ def tile_picked_aqcisendtwo_none_po_kernel(
         h_bank2 = psum.tile([P, H], F32, tag="shared_bank")
         first_product(h_bank2, xq_words1, xq_bytes1[:], 0, H)
         h_sorted1 = keep.tile([P, PACK, P], F32)
-        nc.vector.tensor_scalar_mul(h_sorted1[:], h_bank2[:].rearrange("j (p t) -> j t p", t=PACK), SIXTEENTH)
+        for t in range(PACK):
+            nc.vector.tensor_scalar_mul(
+                h_sorted1[:, t, :], h_bank2[:].rearrange("j (p t) -> j t p", t=PACK)[:, t, :], SIXTEENTH
+            )
         z_bf1 = keep.tile([P, PACK * HALF], BF16, align_bytes=64)
         z_words1 = keep.tile([P, HALF], U32, align_bytes=64)
         z_bytes1 = keep.tile([P, HALF], U8, align_bytes=64)
         turn_and_quantise(1, h_sorted1, z_bf1, z_words1, z_bytes1, HALF)
-        s_second = psum.tile([P, PACK, HALF], F32)
-        for t in range(PACK):
-            second_product(s_second[:, t, :], t, z_words1, z_bytes1, slice(0, HALF))
+        s_next = psum.tile([P, HALF], F32, tag="h_part0")
+        s_last = psum.tile([P, PACK - 1, HALF], F32)
+        second_product(s_next[:], 0, z_words1, z_bytes1, slice(0, HALF))
+        for t in range(1, PACK):
+            second_product(s_last[:, t - 1, :], t, z_words1, z_bytes1, slice(0, HALF))
         s1 = keep.tile([P, PACK, HALF], F32)
-        nc.vector.tensor_scalar_mul(s1[:, 0, :], s_second[:, 0, :], SIXTEENTH)
-        nc.vector.tensor_scalar_mul(s1[:, 1:PACK, :], s_second[:, 1:PACK, :], SIXTEENTH)
+        nc.vector.tensor_scalar_mul(s1[:, 0, :], s_next[:], SIXTEENTH)
+        nc.vector.tensor_scalar_mul(s1[:, 1:PACK, :], s_last[:], SIXTEENTH)
 
         y_bf = keep.tile([P, S * PACK], BF16, align_bytes=64)
         y_dealt = y_bf[:].rearrange("p (c t) -> p c t", t=PACK)

@@ -54,8 +54,8 @@ def tile_picked_aqcisendtwo_none_po_kernel(
         offs_list = load_list(offs, "offs_list")
         x_word_table = keep.tile([P, T], U32, align_bytes=64)
         d_word_table = reuse.tile([P, G], U32, align_bytes=64, offset=0)
-        nc.sync.dma_start(x_word_table[:].bitcast(I32), x_words[0].rearrange("p n t -> p (n t)").bitcast(I32))
         nc.sync.dma_start(d_word_table[:].bitcast(I32), d_words[0].rearrange("p n t -> p (n t)").bitcast(I32))
+        nc.sync.dma_start(x_word_table[:].bitcast(I32), x_words[0].rearrange("p n t -> p (n t)").bitcast(I32))
         cand_list = load_list(cand, "cand_list")
         n_lists = [load_list(n1, "n1_list"), load_list(n2, "n2_list")]
         gs4 = keep.tile([P, PACK], F32)
@@ -68,8 +68,7 @@ def tile_picked_aqcisendtwo_none_po_kernel(
         nc.vector.tensor_copy(d_bytes[:, H : 2 * H], d_byte_table[:].indirect(kb_list[:]))
         nc.vector.tensor_copy(d_bytes[:, 2 * H : 2 * H + HALF], x_block_table[:].indirect(entries(offs_list, 0, HALF)))
         for q in range(4):
-            queue = nc.scalar if q % 2 else nc.sync
-            queue.dma_start(
+            nc.scalar.dma_start(
                 d_plane[32 * q : 32 * q + 4, :].bitcast(I32), d_bytes[32 * q : 32 * q + 32 : 8, :].bitcast(I32)
             )
 
@@ -86,11 +85,6 @@ def tile_picked_aqcisendtwo_none_po_kernel(
         def gather_token_words(half, tile):
             nc.vector.tensor_copy(tile[:], x_word_table[:].indirect(entries(offs_list, half * HALF, HALF)))
 
-        xq_words0 = keep.tile([P, HALF], U32, align_bytes=64)
-        gather_token_words(0, xq_words0)
-        xq_words1 = keep.tile([P, HALF], U32, align_bytes=64)
-        gather_token_words(1, xq_words1)
-
         da_words = keep.tile([P, H], U32, align_bytes=64)
         db_words = keep.tile([P, H], U32, align_bytes=64)
         nc.vector.tensor_copy(da_words[:], d_word_table[:].indirect(ka_list[:]))
@@ -98,6 +92,9 @@ def tile_picked_aqcisendtwo_none_po_kernel(
             nc.vector.tensor_copy(
                 db_words[:, part * 256 : (part + 1) * 256], d_word_table[:].indirect(entries(kb_list, part * 256, 256))
             )
+
+        xq_words0 = reuse.tile([P, HALF], U32, align_bytes=64, offset=4096)
+        gather_token_words(0, xq_words0)
 
         def first_product(bank, words, scale_bytes, lo, n):
             nc.tensor.matmul_mx(
@@ -172,7 +169,9 @@ def tile_picked_aqcisendtwo_none_po_kernel(
             scatter(t, s0[:, t, :], 0, HALF)
 
         xq_bytes1 = reuse.tile([P, HALF], U8, align_bytes=64, offset=8192)
+        xq_words1 = reuse.tile([P, HALF], U32, align_bytes=64, offset=8192 + 256)
         gather_token_bytes(1, xq_bytes1)
+        gather_token_words(1, xq_words1)
         h_bank2 = psum.tile([P, H], F32, tag="shared_bank")
         first_product(h_bank2, xq_words1, xq_bytes1[:], 0, H)
         h_sorted1 = keep.tile([P, PACK, P], F32)

from contextlib import ExitStack

import concourse.mybir as mybir
from concourse.masks import make_identity

K, T, S, G, H, C = 512, 1024, 256, 2048, 512, 512
FLOPS = 2 * (2 * K * H * S) + 2 * H * C * S

F32 = mybir.dt.float32
BF16 = mybir.dt.bfloat16
I32 = mybir.dt.int32
U32 = mybir.dt.uint32
U16 = mybir.dt.uint16
U8 = mybir.dt.uint8
FP8X4 = mybir.dt.float8_e4m3fn_x4
MULT = mybir.AluOpType.mult
MAX = mybir.AluOpType.max
COPY = mybir.ActivationFunctionType.Copy

P = 128
PACK = 4
HALF = S // 2
QUARTER = S // 4
SIXTEENTH = 0.0625


def tile_picked_aqcisendtwo_none_po_kernel(
    tc, x_words, x_scales, d_words, d_scales, gs, offs, ka, kb, cand, n1, n2, out_0, out_1, out_2
):
    nc = tc.nc
    with ExitStack() as ctx:
        lists = ctx.enter_context(tc.tile_pool(name="lists", bufs=1))
        keep = ctx.enter_context(tc.tile_pool(name="keep", bufs=1))
        reuse = ctx.enter_context(tc.tile_pool(name="reuse", bufs=1))
        psum = ctx.enter_context(tc.psum_pool(name="psum", bufs=1))

        def load_list(src, name):
            tile = lists.tile([P, src.shape[1]], U16, name=name)
            nc.sync.dma_start(tile[:], src)
            return tile

        def entries(tile, start, count):
            return tile[:, start // 16 : (start + count) // 16]

        d_byte_table = keep.tile([P, G], U8, align_bytes=64)
        x_block_table = reuse.tile([P, T], U8, align_bytes=64, offset=10240)
        d_plane = keep.tile([P, 2 * H + HALF], U8, align_bytes=64)
        nc.vector.memset(d_plane[:].bitcast(I32), 0)

        nc.sync.dma_start(d_byte_table[:].bitcast(I32), d_scales[0].bitcast(I32).unsqueeze(1).to_broadcast([16, 8, G // 4]))
        ka_list = load_list(ka, "ka_list")
        kb_list = load_list(kb, "kb_list")
        nc.sync.dma_start(x_block_table[:].bitcast(I32), x_scales[0].bitcast(I32).unsqueeze(1).to_broadcast([16, 8, T // 4]))
        offs_list = load_list(offs, "offs_list")
        x_word_table = keep.tile([P, T], U32, align_bytes=64)
        d_word_table = reuse.tile([P, G], U32, align_bytes=64, offset=0)
        nc.sync.dma_start(d_word_table[:].bitcast(I32), d_words[0].rearrange("p n t -> p (n t)").bitcast(I32))
        nc.sync.dma_start(x_word_table[:].bitcast(I32), x_words[0].rearrange("p n t -> p (n t)").bitcast(I32))
        cand_list = load_list(cand, "cand_list")
        n_lists = [load_list(n1, "n1_list"), load_list(n2, "n2_list")]
        gs4 = keep.tile([P, PACK], F32)
        nc.gpsimd.dma_start(gs4[:], gs.rearrange("(p t) o -> p (t o)", t=PACK))
        ident = keep.tile([P, P], F32)
        make_identity(nc, ident[:])

        d_bytes = keep.tile([P, 2 * H + HALF], U8, align_bytes=64)
        nc.vector.tensor_copy(d_bytes[:, 0:H], d_byte_table[:].indirect(ka_list[:]))
        nc.vector.tensor_copy(d_bytes[:, H : 2 * H], d_byte_table[:].indirect(kb_list[:]))
        nc.vector.tensor_copy(d_bytes[:, 2 * H : 2 * H + HALF], x_block_table[:].indirect(entries(offs_list, 0, HALF)))
        for q in range(4):
            nc.scalar.dma_start(
                d_plane[32 * q : 32 * q + 4, :].bitcast(I32), d_bytes[32 * q : 32 * q + 32 : 8, :].bitcast(I32)
            )

        x_byte_table = reuse.tile([P, T], U8, align_bytes=64, offset=10240)
        for q in range(4):
            nc.sync.dma_start(
                x_byte_table[32 * q : 32 * q + 32, :].bitcast(I32),
                x_scales[0, 4 * q : 4 * q + 4, :].bitcast(I32).unsqueeze(0).to_broadcast([8, 4, T // 4]),
            )

        def gather_token_bytes(half, tile):
            nc.vector.tensor_copy(tile[:], x_byte_table[:].indirect(entries(offs_list, half * HALF, HALF)))

        def gather_token_words(half, tile):
            nc.vector.tensor_copy(tile[:], x_word_table[:].indirect(entries(offs_list, half * HALF, HALF)))

        da_words = keep.tile([P, H], U32, align_bytes=64)
        db_words = keep.tile([P, H], U32, align_bytes=64)
        nc.vector.tensor_copy(da_words[:], d_word_table[:].indirect(ka_list[:]))
        for part in range(2):
            nc.vector.tensor_copy(
                db_words[:, part * 256 : (part + 1) * 256], d_word_table[:].indirect(entries(kb_list, part * 256, 256))
            )

        xq_words0 = reuse.tile([P, HALF], U32, align_bytes=64, offset=4096)
        gather_token_words(0, xq_words0)

        def first_product(bank, words, scale_bytes, lo, n):
            nc.tensor.matmul_mx(
                bank[:, 0:n], lhsT=words[:].bitcast(FP8X4), lhsT_scale=scale_bytes,
                rhs=da_words[:, lo : lo + n].bitcast(FP8X4), rhs_scale=d_plane[:, lo : lo + n], start=True, stop=False,
            )
            nc.tensor.matmul_mx(
                bank[:, 0:n], lhsT=words[:].bitcast(FP8X4), lhsT_scale=scale_bytes,
                rhs=db_words[:, lo : lo + n].bitcast(FP8X4), rhs_scale=d_plane[:, H + lo : H + lo + n],
                start=False, stop=True,
            )

        h_sorted0 = keep.tile([P, PACK, P], F32)
        for part in range(2):
            bank = psum.tile([P, 256], F32, name="h_bank%d" % part, tag="h_part%d" % part)
            first_product(bank, xq_words0, d_plane[:, 2 * H : 2 * H + HALF], part * 256, 256)
            nc.scalar.activation(
                h_sorted0[:, :, part * 64 : (part + 1) * 64], bank[:].rearrange("j (p t) -> j t p", t=PACK),
                COPY, scale=SIXTEENTH,
            )

        c_bytes = reuse.tile([P, C], U8, align_bytes=64, offset=2048)
        c_words = reuse.tile([P, C], U32, align_bytes=64, offset=0)
        nc.vector.tensor_copy(c_words[:].rearrange("p (t m) -> p m t", t=PACK), x_word_table[:].indirect(cand_list[:]))
        nc.vector.tensor_copy(c_bytes[:].rearrange("p (t m) -> p m t", t=PACK), x_byte_table[:].indirect(cand_list[:]))

        def turn_and_quantise(half, h_sorted, z_bf, z_words, z_bytes, width):
            turned = psum.tile([P, PACK, HALF], F32, name="turned%d" % half)
            for t in range(PACK):
                nc.tensor.transpose(turned[:, t, :], h_sorted[:, t, :], ident[:])
            gs_spread = gs4[:].unsqueeze(1).to_broadcast([P, width, PACK])
            for lo in range(0, HALF, width):
                nc.vector.tensor_tensor(
                    z_bf[:, PACK * lo : PACK * (lo + width)].rearrange("p (j t) -> p j t", t=PACK),
                    turned[:, :, lo : lo + width].rearrange("p t j -> p j t"), gs_spread, MULT,
                )
            for lo in range(0, HALF, width):
                nc.vector.quantize_mx(
                    z_words[:, lo : lo + width].bitcast(FP8X4), z_bytes[:, lo : lo + width],
                    z_bf[:, PACK * lo : PACK * (lo + width)],
                )

        def second_product(out, t, z_words, z_bytes, cols):
            nc.tensor.matmul_mx(
                out, lhsT=c_words[:, t * P : (t + 1) * P].bitcast(FP8X4), lhsT_scale=c_bytes[:, t * P : (t + 1) * P],
                rhs=z_words[:, cols].bitcast(FP8X4), rhs_scale=z_bytes[:, cols], start=True, stop=True,
            )

        ds = [[keep.tile([P, S], F32, name="ds%d_%d" % (t, w)) for w in range(2)] for t in range(PACK)]

        def scatter(t, values, start, count):
            for w in range(2):
                nc.scalar.activation(ds[t][w][:].indirect(entries(n_lists[w], start, count)), values, COPY)

        z_bf0 = reuse.tile([P, PACK * HALF], BF16, align_bytes=64, offset=8192)
        z_words0 = keep.tile([P, HALF], U32, align_bytes=64)
        z_bytes0 = keep.tile([P, HALF], U8, align_bytes=64)
        turn_and_quantise(0, h_sorted0, z_bf0, z_words0, z_bytes0, QUARTER)
        s0 = keep.tile([P, PACK, HALF], F32)
        s_lead = [psum.tile([P, QUARTER], F32, name="s_lead0", tag="shared_bank"), psum.tile([P, QUARTER], F32, name="s_lead1")]
        s_rest = psum.tile([P, PACK - 1, HALF], F32)
        for u in range(2):
            second_product(s_lead[u][:], 0, z_words0, z_bytes0, slice(u * QUARTER, (u + 1) * QUARTER))
        for t in range(1, PACK):
            second_product(s_rest[:, t - 1, :], t, z_words0, z_bytes0, slice(0, HALF))
        for u in range(2):
            nc.vector.tensor_scalar_mul(s0[:, 0, u * QUARTER : (u + 1) * QUARTER], s_lead[u][:], SIXTEENTH)
        nc.vector.tensor_scalar_mul(s0[:, 1:PACK, :], s_rest[:], SIXTEENTH)
        for u in range(2):
            scatter(0, s0[:, 0, u * QUARTER : (u + 1) * QUARTER], u * QUARTER, QUARTER)
        for t in range(1, PACK):
            scatter(t, s0[:, t, :], 0, HALF)

        xq_bytes1 = reuse.tile([P, HALF], U8, align_bytes=64, offset=8192)
        xq_words1 = reuse.tile([P, HALF], U32, align_bytes=64, offset=8192 + 256)
        gather_token_bytes(1, xq_bytes1)
        gather_token_words(1, xq_words1)
        h_bank2 = psum.tile([P, H], F32, tag="shared_bank")
        first_product(h_bank2, xq_words1, xq_bytes1[:], 0, H)
        h_sorted1 = keep.tile([P, PACK, P], F32)
        for t in range(PACK):
            nc.vector.tensor_scalar_mul(
                h_sorted1[:, t, :], h_bank2[:].rearrange("j (p t) -> j t p", t=PACK)[:, t, :], SIXTEENTH
            )
        z_bf1 = keep.tile([P, PACK * HALF], BF16, align_bytes=64)
        z_words1 = keep.tile([P, HALF], U32, align_bytes=64)
        z_bytes1 = keep.tile([P, HALF], U8, align_bytes=64)
        turn_and_quantise(1, h_sorted1, z_bf1, z_words1, z_bytes1, HALF)
        s_next = psum.tile([P, HALF], F32, tag="h_part0")
        s_last = psum.tile([P, PACK - 1, HALF], F32)
        second_product(s_next[:], 0, z_words1, z_bytes1, slice(0, HALF))
        for t in range(1, PACK):
            second_product(s_last[:, t - 1, :], t, z_words1, z_bytes1, slice(0, HALF))
        s1 = keep.tile([P, PACK, HALF], F32)
        nc.vector.tensor_scalar_mul(s1[:, 0, :], s_next[:], SIXTEENTH)
        nc.vector.tensor_scalar_mul(s1[:, 1:PACK, :], s_last[:], SIXTEENTH)

        y_bf = keep.tile([P, S * PACK], BF16, align_bytes=64)
        y_dealt = y_bf[:].rearrange("p (c t) -> p c t", t=PACK)
        out_rows = out_0.rearrange("(p t) c -> p t c", t=PACK)
        halves = [slice(0, HALF), slice(HALF, S)]
        for t in range(PACK):
            scatter(t, s1[:, t, :], HALF, HALF)
            y = keep.tile([P, S], F32, name="y%d" % t)
            for cols in halves:
                nc.vector.tensor_tensor(y[:, cols], ds[t][0][:, cols], ds[t][1][:, cols], MAX)
            nc.sync.dma_start(out_rows[:, t, :], y[:])
            for cols in halves:
                nc.vector.tensor_copy(y_dealt[:, cols, t], y[:, cols])

        y_words = keep.tile([P, S], U32, align_bytes=64)
        y_bytes = keep.tile([P, S], U8, align_bytes=64)
        for cols in halves:
            nc.vector.quantize_mx(
                y_words[:, cols].bitcast(FP8X4), y_bytes[:, cols], y_bf[:, PACK * cols.start : PACK * cols.stop]
            )
            nc.sync.dma_start(
                out_1[0].rearrange("p n t -> p (n t)").bitcast(I32)[:, cols], y_words[:, cols].bitcast(I32)
            )
        for q in range(4):
            queue = nc.scalar if q < 2 else nc.sync
            queue.dma_start(out_2[0, 4 * q : 4 * q + 4, :].bitcast(I32), y_bytes[32 * q : 32 * q + 4, :].bitcast(I32))
